import numpy as np
import ml_dtypes


def mxq(x, axis, fmt="e4m3"):
    dtype, down = {"e4m3": (ml_dtypes.float8_e4m3fn, 7), "e5m2": (ml_dtypes.float8_e5m2, 14)}[fmt]
    v = np.moveaxis(np.asarray(x, np.float32).astype(ml_dtypes.bfloat16).astype(np.float64), axis, -1)
    blocks = v.reshape(v.shape[:-1] + (-1, 32))
    amax = np.abs(blocks).max(-1, keepdims=True)
    byte = np.maximum(np.where(amax > 0, np.frexp(amax)[1] - 1 + 127, 0) - down, 1)
    scale = np.exp2(byte - 127.0)
    codes = (blocks / scale).astype(np.float32).astype(dtype).astype(np.float64)
    return np.moveaxis((codes * scale).reshape(v.shape), -1, axis)


WIDE = False


def mx_kscale(k):
    if not WIDE:
        return np.ones(k)
    levels = np.array([10, -10, 5, -5, 0])
    if k % 512:
        return np.exp2(np.random.permutation(np.resize(levels, k // 32))).repeat(32)
    a = np.empty((k // 512, 16))
    for p in range(k // 512):
        a[p, :8] = np.random.permutation(np.resize(levels, 8))
        for g in range(8):
            far = levels[np.abs(levels - a[p, g]) >= 10]
            a[p, g + 8] = far[np.random.randint(len(far))]
    return np.exp2(a.ravel()).repeat(32)


def f64(x):
    return np.asarray(x).astype(np.float64)


def striped(idx):
    return np.tile(np.asarray(idx).reshape(-1, 16).T, (8, 1)).astype(np.uint16)


def unstriped(offs):
    return offs[:16].T.reshape(-1).astype(np.int64)


E2M1 = np.array([0.0, 0.5, 1.0, 1.5, 2.0, 3.0, 4.0, 6.0, -0.0, -0.5, -1.0, -1.5, -2.0, -3.0, -4.0, -6.0])


def pack_weight(w, fmt):
    k, n = w.shape
    w = f64(np.asarray(w, np.float32).astype(ml_dtypes.bfloat16)).reshape(k // 32, 32, n)
    amax = np.abs(w).max(1)
    if fmt == "e4m3":
        byte = np.frexp(amax)[1] - 1 + 127 - 7
    else:
        mant, ex = np.frexp(amax / 6.0)
        byte = np.where(mant > 0.5, ex, ex - 1) + 127
    byte = np.clip(np.where(amax > 0, byte, 1), 1, 254)
    scaled = (w * np.exp2(127.0 - byte)[:, None, :]).reshape(k, n).astype(np.float32)
    by_word = np.ascontiguousarray(scaled.reshape(k // 512, 128, 4, n).transpose(0, 1, 3, 2))
    if fmt == "e4m3":
        words = by_word.astype(ml_dtypes.float8_e4m3fn).view(np.uint8)
    else:
        c = by_word.astype(ml_dtypes.float4_e2m1fn).view(np.uint8) & 0xF
        words = (c[..., 0::2] | (c[..., 1::2] << 4)).reshape(k // 512, 128, 2 * n)
    return np.ascontiguousarray(words), np.ascontiguousarray(byte.astype(np.uint8).reshape(k // 512, 16, n))


def unpack_weight(words, scales, fmt):
    g, _, n = scales.shape
    words = np.ascontiguousarray(words).reshape(g, 128, n, -1)
    if fmt == "e4m3":
        vals = words.view(ml_dtypes.float8_e4m3fn).astype(np.float64)
    else:
        nib = np.empty((g, 128, n, 4), np.uint8)
        nib[..., 0::2] = words & 0xF
        nib[..., 1::2] = words >> 4
        vals = E2M1[nib]
    vals = vals * np.repeat(np.exp2(scales.astype(np.float64) - 127.0), 8, axis=1)[..., None]
    return vals.transpose(0, 1, 3, 2).reshape(g * 512, n)


def softplus(v):
    return np.log(1.0 + np.exp(v))


def bf(x):
    return np.asarray(x, np.float32).astype(ml_dtypes.bfloat16)


def planes(Y):
    r, m = Y.shape
    b = f64(bf(Y)).reshape(r // 32, 32, m)
    amax = np.abs(b).max(1)
    byte = np.clip(np.where(amax > 0, np.frexp(amax)[1] - 1 + 127 - 7, 1), 1, 254)
    codes = (b * np.exp2(127.0 - byte)[:, None, :]).reshape(r, m).astype(np.float32).astype(ml_dtypes.float8_e4m3fn).view(np.uint8)
    words = codes.reshape(r // 512, 128, 4, m).transpose(0, 1, 3, 2)
    return np.ascontiguousarray(words), np.ascontiguousarray(byte.astype(np.uint8).reshape(r // 512, 16, m))


K, L, T, J, N = 1024, 512, 1024, 512, 512


def setup_inputs():
    n = np.random.standard_normal
    idx = np.random.permutation(T)[:J]
    fk = mx_kscale(K)
    fl = mx_kscale(L)
    xtp = pack_weight(n((K, T)) / fk[:, None], "e2m1")
    xep = pack_weight(n((L, J)) / fl[:, None], "e4m3")
    wep = pack_weight(n((L, N)) * 1 / np.sqrt(L) * fl[:, None], "e2m1")
    return {
        "xt_words": xtp[0],
        "xt_scales": xtp[1],
        "ws": (n((K, N)) * 1 / np.sqrt(K) * fk[:, None]).astype(np.float32),
        "xe_words": xep[0],
        "xe_scales": xep[1],
        "we_words": wep[0],
        "we_scales": wep[1],
        "b": (np.random.uniform(-0.5, 0.5, (N, 1))).astype(np.float32),
        "offs": striped(idx),
    }


def reference(xt_words, xt_scales, ws, xe_words, xe_scales, we_words, we_scales, b, offs):
    idx = unstriped(offs)
    xtu = unpack_weight(xt_words, xt_scales, "e2m1")
    xeu = unpack_weight(xe_words, xe_scales, "e4m3")
    weu = unpack_weight(we_words, we_scales, "e2m1")
    wsq = mxq(f64(ws), 0, "e4m3")
    u = wsq.T @ xtu
    p = weu.T @ xeu
    d = softplus(p - u[:, idx])
    dp = np.zeros((N, T))
    dp[:, idx] = d
    y = u + dp + f64(b)
    words, scales = planes(y)
    return y, words, scales

@@ -1,0 +1,231 @@
+from contextlib import ExitStack
+
+import concourse.mybir as mybir
+
+K, L, T, J, N = 1024, 512, 1024, 512, 512
+FLOPS = 2 * K * N * T + 2 * L * N * J
+
+F32 = mybir.dt.float32
+BF16 = mybir.dt.bfloat16
+I32 = mybir.dt.int32
+U32 = mybir.dt.uint32
+U16 = mybir.dt.uint16
+U8 = mybir.dt.uint8
+FP8X4 = mybir.dt.float8_e4m3fn_x4
+FP4X4 = mybir.dt.float4_e2m1fn_x4
+ACT = mybir.ActivationFunctionType
+ALU = mybir.AluOpType
+
+P = 128
+PACK = 4
+BANK = 512
+PASSES = K // (P * PACK)
+WCH = 2
+QUARTERS = 4
+
+
+def tile_moe_smooth_larger_of_expert_and_shared_pl_kernel(
+    tc, xt_words, xt_scales, ws, xe_words, xe_scales, we_words, we_scales, b, offs, out_0, out_1, out_2
+):
+    nc = tc.nc
+    with ExitStack() as ctx:
+        held = ctx.enter_context(tc.tile_pool(name="held", bufs=1))
+        ring = ctx.enter_context(tc.tile_pool(name="ring", bufs=2))
+        psum = ctx.enter_context(tc.psum_pool(name="psum", bufs=1))
+
+        offsets = held.tile([P, J // 16], U16, name="offsets")
+        bias = held.tile([P, PACK], F32, name="bias")
+        xt_w = held.tile([P, PASSES, 2 * T], U8, name="xt_w", align_bytes=64)
+        xt_s = held.tile([P, PASSES, T], U8, name="xt_s", align_bytes=64)
+        xe_w = held.tile([P, J], U32, name="xe_w", align_bytes=64)
+        xe_s = held.tile([P, J], U8, name="xe_s", align_bytes=64)
+        we_w_raw = held.tile([P, 2 * N], U8, name="we_w_raw", align_bytes=64)
+        we_s_raw = held.tile([P, N], U8, name="we_s_raw", align_bytes=64)
+        we_w = held.tile([P, 2 * N], U8, name="we_w", align_bytes=64)
+        we_s = held.tile([P, N], U8, name="we_s", align_bytes=64)
+        cw = N // WCH
+        ws_raw = [[held.tile([P, PACK, cw], F32, name=f"ws_raw{g}{h}") for h in range(WCH)] for g in range(PASSES)]
+        ws_bf = [[held.tile([P, 2 * P * PACK], BF16, name=f"ws_bf{g}{a}", align_bytes=64) for a in range(2)] for g in range(PASSES)]
+        ws_w = [[held.tile([P, 2 * P], U32, name=f"ws_w{g}{a}", align_bytes=64) for a in range(2)] for g in range(PASSES)]
+        ws_s = [[held.tile([P, 2 * P], U8, name=f"ws_s{g}{a}", align_bytes=64) for a in range(2)] for g in range(PASSES)]
+        p_sb = [held.tile([P, J], F32, name=f"p_sb{t}") for t in range(PACK)]
+        u_sb = [held.tile([P, T], F32, name=f"u_sb{t}") for t in range(PACK)]
+        z_sb = [held.tile([P, J], F32, name=f"z_sb{t}") for t in range(PACK)]
+        dp = [held.tile([P, T], F32, name=f"dp{t}") for t in range(PACK)]
+        y = held.tile([P, PACK, T], F32, name="y")
+        qw = T // QUARTERS
+        y_bf = [held.tile([P, qw * PACK], BF16, name=f"y_bf{q}", align_bytes=64) for q in range(QUARTERS)]
+        y_w = held.tile([P, T], U32, name="y_w", align_bytes=64)
+        y_s = held.tile([P, T], U8, name="y_s", align_bytes=64)
+
+        nc.vector.memset(we_s_raw[:].bitcast(I32), 0)
+        nc.vector.memset(xe_s[:].bitcast(I32), 0)
+        nc.vector.memset(xt_s[:].rearrange("p g c -> p (g c)").bitcast(I32), 0)
+
+        def load_ws(g, h):
+            rows = ws[g * P * PACK : (g + 1) * P * PACK, h * cw : (h + 1) * cw]
+            nc.sync.dma_start(out=ws_raw[g][h][:], in_=rows.rearrange("(p j) c -> p j c", j=PACK))
+
+        def load_scales(tile, src):
+            for q in range(4):
+                nc.sync.dma_start(out=tile[32 * q : 32 * q + 4].bitcast(I32), in_=src[4 * q : 4 * q + 4].bitcast(I32))
+
+        nc.gpsimd.dma_start(out=bias[:], in_=b.rearrange("(p t) o -> p (t o)", t=PACK))
+        nc.sync.dma_start(out=we_w_raw[:].bitcast(I32), in_=we_words[0].bitcast(I32))
+        load_ws(0, 0)
+        load_scales(we_s_raw, we_scales[0])
+        load_ws(0, 1)
+        nc.sync.dma_start(out=xe_w[:].bitcast(I32), in_=xe_words[0].rearrange("p c r -> p (c r)").bitcast(I32))
+        load_scales(xe_s, xe_scales[0])
+        nc.sync.dma_start(out=xt_w[:].bitcast(I32), in_=xt_words.rearrange("g p c -> p g c").bitcast(I32))
+        load_ws(1, 0)
+        load_scales(xt_s, xt_scales.rearrange("g q c -> q g c"))
+        load_ws(1, 1)
+        nc.sync.dma_start(offsets[:], offs)
+
+        for t in range(PACK):
+            nc.vector.memset(dp[t][:], 0.0)
+
+        nc.vector.tensor_copy(
+            out=we_w[:].rearrange("p (t m e) -> p t m e", t=PACK, e=2),
+            in_=we_w_raw[:].rearrange("p (m t e) -> p t m e", t=PACK, e=2),
+        )
+        nc.vector.tensor_copy(
+            out=we_s[:].rearrange("p (t m) -> p t m", t=PACK),
+            in_=we_s_raw[:].rearrange("p (m t) -> p t m", t=PACK),
+        )
+
+        def round_ws(g, h):
+            mw = cw // PACK
+            src = ws_raw[g][h][:].rearrange("p j (m t) -> p m j t", t=PACK)
+            for a in range(2):
+                dst = ws_bf[g][a][:].rearrange("p (t m j) -> p m j t", t=2, j=PACK)[:, h * mw : (h + 1) * mw]
+                if a == 0:
+                    nc.vector.tensor_copy(out=dst, in_=src[:, :, :, 0:2])
+                else:
+                    nc.scalar.copy(out=dst, in_=src[:, :, :, 2:4])
+
+        def quantize_ws(g, a):
+            nc.vector.quantize_mx(out=ws_w[g][a][:].bitcast(FP8X4), scales=ws_s[g][a][:], in_=ws_bf[g][a][:])
+
+        round_ws(0, 0)
+        round_ws(0, 1)
+        quantize_ws(0, 0)
+        quantize_ws(0, 1)
+
+        for t in range(PACK):
+            acc = psum.tile([P, BANK], F32, name=f"p_acc{t}", tag=f"bank{4 + t}")
+            nc.tensor.matmul_mx(
+                out=acc[:],
+                lhsT=we_w[:, 2 * P * t : 2 * P * (t + 1)].bitcast(FP4X4),
+                lhsT_scale=we_s[:, P * t : P * (t + 1)],
+                rhs=xe_w[:].bitcast(FP8X4),
+                rhs_scale=xe_s[:],
+                start=True,
+                stop=True,
+            )
+            nc.scalar.copy(out=p_sb[t][:], in_=acc[:])
+
+        u_acc = [[psum.tile([P, BANK], F32, name=f"u_acc{t}{h}", tag=f"bank{2 * t + h}") for h in range(2)] for t in range(PACK)]
+
+        def u_pass(g, t, h):
+            a, i = divmod(t, 2)
+            nc.tensor.matmul_mx(
+                out=u_acc[t][h][:],
+                lhsT=ws_w[g][a][:, P * i : P * (i + 1)].bitcast(FP8X4),
+                lhsT_scale=ws_s[g][a][:, P * i : P * (i + 1)],
+                rhs=xt_w[:, g, 2 * BANK * h : 2 * BANK * (h + 1)].bitcast(FP4X4),
+                rhs_scale=xt_s[:, g, BANK * h : BANK * (h + 1)],
+                start=(g == 0),
+                stop=(g == PASSES - 1),
+            )
+
+        for t in range(PACK):
+            for h in range(2):
+                u_pass(0, t, h)
+
+        round_ws(1, 0)
+        round_ws(1, 1)
+        quantize_ws(1, 0)
+        quantize_ws(1, 1)
+        for t in range(PACK):
+            for h in range(2):
+                u_pass(1, t, h)
+
+        def empty_u(t, h, on_vector):
+            dst = u_sb[t][:, BANK * h : BANK * (h + 1)]
+            if on_vector:
+                nc.vector.tensor_copy(out=dst, in_=u_acc[t][h][:])
+            else:
+                nc.scalar.copy(out=dst, in_=u_acc[t][h][:])
+
+        def gather(t):
+            nc.vector.tensor_tensor(z_sb[t][:], u_sb[t][:].indirect(offsets[:]), p_sb[t][:], ALU.subtract)
+
+        empty_u(0, 0, False)
+        empty_u(0, 1, True)
+        empty_u(1, 0, False)
+        empty_u(1, 1, False)
+        gather(0)
+        gather(1)
+        for t in (2, 3):
+            empty_u(t, 0, True)
+            empty_u(t, 1, True)
+            gather(t)
+
+        out_rows = out_0.rearrange("(p t) c -> p t c", t=PACK)
+
+        def add(t, cols):
+            nc.vector.scalar_tensor_tensor(
+                out=y[:, t, cols], in0=u_sb[t][:, cols], scalar=bias[:, t : t + 1], in1=dp[t][:, cols], op0=ALU.add, op1=ALU.add
+            )
+
+        for a in range(2):
+            mag = held.tile([P, 2 * J], F32, name=f"mag{a}", tag="mag")
+            ex = held.tile([P, 2 * J], F32, name=f"ex{a}", tag="ex")
+            for i in range(2):
+                nc.scalar.activation(out=mag[:, J * i : J * (i + 1)], in_=z_sb[2 * a + i][:], func=ACT.Abs)
+            nc.scalar.activation(out=ex[:], in_=mag[:], func=ACT.Exp, scale=-1.0)
+            for i in range(2):
+                t = 2 * a + i
+                tail = ring.tile([P, J], F32, name=f"tail{t}", tag="tail")
+                lin = ring.tile([P, J], F32, name=f"lin{t}", tag="lin")
+                nc.scalar.activation(out=tail[:], in_=ex[:, J * i : J * (i + 1)], func=ACT.Ln, bias=1.0)
+                nc.scalar.activation(out=lin[:], in_=z_sb[t][:], func=ACT.Relu, scale=-1.0)
+                nc.vector.tensor_tensor(dp[t][:].indirect(offsets[:]), tail[:], lin[:], ALU.add)
+                if t < PACK - 1:
+                    add(t, slice(0, T))
+                    nc.sync.dma_start(out=out_rows[:, t, :], in_=y[:, t, :])
+
+        last = PACK - 1
+        for q in range(QUARTERS):
+            add(last, slice(q * qw, (q + 1) * qw))
+            if q % 2 == 1:
+                cols = slice((q - 1) * qw, (q + 1) * qw)
+                nc.sync.dma_start(out=out_rows[:, last, cols], in_=y[:, last, cols])
+
+        def round_y(q):
+            src = y[:, :, q * qw : (q + 1) * qw].rearrange("p t (c i) -> p c t i", i=4)
+            dst = y_bf[q][:].rearrange("p (c i t) -> p c t i", i=4, t=PACK)
+            if q < 2:
+                nc.scalar.copy(out=dst, in_=src)
+            else:
+                nc.vector.tensor_copy(out=dst, in_=src)
+
+        words_out = out_1[0].rearrange("p c r -> p (c r)").bitcast(I32)
+
+        def quantize_y(q):
+            cols = slice(q * qw, (q + 1) * qw)
+            nc.vector.quantize_mx(out=y_w[:, cols].bitcast(FP8X4), scales=y_s[:, cols], in_=y_bf[q][:])
+            nc.sync.dma_start(out=words_out[:, cols], in_=y_w[:, cols].bitcast(I32))
+
+        round_y(0)
+        round_y(1)
+        round_y(2)
+        quantize_y(0)
+        round_y(3)
+        quantize_y(2)
+        quantize_y(1)
+        quantize_y(3)
+        for q in range(4):
+            nc.scalar.dma_start(out=out_2[0, 4 * q : 4 * q + 4, :].bitcast(I32), in_=y_s[32 * q : 32 * q + 4, :].bitcast(I32))

@@ -20,7 +20,6 @@ P = 128
 PACK = 4
 BANK = 512
 PASSES = K // (P * PACK)
-WCH = 2
 QUARTERS = 4
 
 
@@ -43,8 +42,7 @@ def tile_moe_smooth_larger_of_expert_and_shared_pl_kernel(
         we_s_raw = held.tile([P, N], U8, name="we_s_raw", align_bytes=64)
         we_w = held.tile([P, 2 * N], U8, name="we_w", align_bytes=64)
         we_s = held.tile([P, N], U8, name="we_s", align_bytes=64)
-        cw = N // WCH
-        ws_raw = [[held.tile([P, PACK, cw], F32, name=f"ws_raw{g}{h}") for h in range(WCH)] for g in range(PASSES)]
+        ws_raw = [held.tile([P, PACK, N], F32, name=f"ws_raw{g}") for g in range(PASSES)]
         ws_bf = [[held.tile([P, 2 * P * PACK], BF16, name=f"ws_bf{g}{a}", align_bytes=64) for a in range(2)] for g in range(PASSES)]
         ws_w = [[held.tile([P, 2 * P], U32, name=f"ws_w{g}{a}", align_bytes=64) for a in range(2)] for g in range(PASSES)]
         ws_s = [[held.tile([P, 2 * P], U8, name=f"ws_s{g}{a}", align_bytes=64) for a in range(2)] for g in range(PASSES)]
@@ -58,29 +56,27 @@ def tile_moe_smooth_larger_of_expert_and_shared_pl_kernel(
         y_w = held.tile([P, T], U32, name="y_w", align_bytes=64)
         y_s = held.tile([P, T], U8, name="y_s", align_bytes=64)
 
-        nc.vector.memset(we_s_raw[:].bitcast(I32), 0)
-        nc.vector.memset(xe_s[:].bitcast(I32), 0)
-        nc.vector.memset(xt_s[:].rearrange("p g c -> p (g c)").bitcast(I32), 0)
+        nc.gpsimd.memset(we_s_raw[:].bitcast(I32), 0)
+        nc.gpsimd.memset(xe_s[:].bitcast(I32), 0)
+        nc.gpsimd.memset(xt_s[:].rearrange("p g c -> p (g c)").bitcast(I32), 0)
 
-        def load_ws(g, h):
-            rows = ws[g * P * PACK : (g + 1) * P * PACK, h * cw : (h + 1) * cw]
-            nc.sync.dma_start(out=ws_raw[g][h][:], in_=rows.rearrange("(p j) c -> p j c", j=PACK))
+        def load_ws(g):
+            rows = ws[g * P * PACK : (g + 1) * P * PACK, :]
+            nc.sync.dma_start(out=ws_raw[g][:], in_=rows.rearrange("(p j) c -> p j c", j=PACK))
 
         def load_scales(tile, src):
             for q in range(4):
                 nc.sync.dma_start(out=tile[32 * q : 32 * q + 4].bitcast(I32), in_=src[4 * q : 4 * q + 4].bitcast(I32))
 
-        nc.gpsimd.dma_start(out=bias[:], in_=b.rearrange("(p t) o -> p (t o)", t=PACK))
         nc.sync.dma_start(out=we_w_raw[:].bitcast(I32), in_=we_words[0].bitcast(I32))
-        load_ws(0, 0)
         load_scales(we_s_raw, we_scales[0])
-        load_ws(0, 1)
         nc.sync.dma_start(out=xe_w[:].bitcast(I32), in_=xe_words[0].rearrange("p c r -> p (c r)").bitcast(I32))
-        load_scales(xe_s, xe_scales[0])
         nc.sync.dma_start(out=xt_w[:].bitcast(I32), in_=xt_words.rearrange("g p c -> p g c").bitcast(I32))
-        load_ws(1, 0)
+        load_ws(0)
+        load_scales(xe_s, xe_scales[0])
+        nc.sync.dma_start(out=bias[:], in_=b.rearrange("(p t) o -> p (t o)", t=PACK))
+        load_ws(1)
         load_scales(xt_s, xt_scales.rearrange("g q c -> q g c"))
-        load_ws(1, 1)
         nc.sync.dma_start(offsets[:], offs)
 
         for t in range(PACK):
@@ -95,23 +91,25 @@ def tile_moe_smooth_larger_of_expert_and_shared_pl_kernel(
             in_=we_s_raw[:].rearrange("p (m t) -> p t m", t=PACK),
         )
 
-        def round_ws(g, h):
-            mw = cw // PACK
-            src = ws_raw[g][h][:].rearrange("p j (m t) -> p m j t", t=PACK)
+        def round_ws(g):
+            src = ws_raw[g][:].rearrange("p j (m t) -> p m j t", t=PACK)
             for a in range(2):
-                dst = ws_bf[g][a][:].rearrange("p (t m j) -> p m j t", t=2, j=PACK)[:, h * mw : (h + 1) * mw]
+                dst = ws_bf[g][a][:].rearrange("p (t m j) -> p m j t", t=2, j=PACK)
                 if a == 0:
                     nc.vector.tensor_copy(out=dst, in_=src[:, :, :, 0:2])
                 else:
                     nc.scalar.copy(out=dst, in_=src[:, :, :, 2:4])
 
-        def quantize_ws(g, a):
-            nc.vector.quantize_mx(out=ws_w[g][a][:].bitcast(FP8X4), scales=ws_s[g][a][:], in_=ws_bf[g][a][:])
+        def quantize_ws(g, t):
+            a, i = divmod(t, 2)
+            cols = slice(P * i, P * (i + 1))
+            nc.vector.quantize_mx(
+                out=ws_w[g][a][:, cols].bitcast(FP8X4), scales=ws_s[g][a][:, cols], in_=ws_bf[g][a][:, PACK * P * i : PACK * P * (i + 1)]
+            )
 
-        round_ws(0, 0)
-        round_ws(0, 1)
-        quantize_ws(0, 0)
-        quantize_ws(0, 1)
+        round_ws(0)
+        for t in range(PACK):
+            quantize_ws(0, t)
 
         for t in range(PACK):
             acc = psum.tile([P, BANK], F32, name=f"p_acc{t}", tag=f"bank{4 + t}")
@@ -124,7 +122,7 @@ def tile_moe_smooth_larger_of_expert_and_shared_pl_kernel(
                 start=True,
                 stop=True,
             )
-            nc.scalar.copy(out=p_sb[t][:], in_=acc[:])
+            nc.scalar.activation(out=p_sb[t][:], in_=acc[:], func=ACT.Identity, bias=bias[:, t : t + 1])
 
         u_acc = [[psum.tile([P, BANK], F32, name=f"u_acc{t}{h}", tag=f"bank{2 * t + h}") for h in range(2)] for t in range(PACK)]
 
@@ -140,24 +138,20 @@ def tile_moe_smooth_larger_of_expert_and_shared_pl_kernel(
                 stop=(g == PASSES - 1),
             )
 
+        round_ws(1)
         for t in range(PACK):
-            for h in range(2):
-                u_pass(0, t, h)
-
-        round_ws(1, 0)
-        round_ws(1, 1)
-        quantize_ws(1, 0)
-        quantize_ws(1, 1)
+            quantize_ws(1, t)
         for t in range(PACK):
-            for h in range(2):
-                u_pass(1, t, h)
+            for g in range(PASSES):
+                for h in range(2):
+                    u_pass(g, t, h)
 
         def empty_u(t, h, on_vector):
             dst = u_sb[t][:, BANK * h : BANK * (h + 1)]
             if on_vector:
-                nc.vector.tensor_copy(out=dst, in_=u_acc[t][h][:])
+                nc.vector.tensor_scalar(out=dst, in0=u_acc[t][h][:], scalar1=bias[:, t : t + 1], scalar2=None, op0=ALU.add)
             else:
-                nc.scalar.copy(out=dst, in_=u_acc[t][h][:])
+                nc.scalar.activation(out=dst, in_=u_acc[t][h][:], func=ACT.Identity, bias=bias[:, t : t + 1])
 
         def gather(t):
             nc.vector.tensor_tensor(z_sb[t][:], u_sb[t][:].indirect(offsets[:]), p_sb[t][:], ALU.subtract)
@@ -175,10 +169,8 @@ def tile_moe_smooth_larger_of_expert_and_shared_pl_kernel(
 
         out_rows = out_0.rearrange("(p t) c -> p t c", t=PACK)
 
-        def add(t, cols):
-            nc.vector.scalar_tensor_tensor(
-                out=y[:, t, cols], in0=u_sb[t][:, cols], scalar=bias[:, t : t + 1], in1=dp[t][:, cols], op0=ALU.add, op1=ALU.add
-            )
+        def add(engine, t, cols):
+            engine.tensor_tensor(y[:, t, cols], u_sb[t][:, cols], dp[t][:, cols], ALU.subtract)
 
         for a in range(2):
             mag = held.tile([P, 2 * J], F32, name=f"mag{a}", tag="mag")
@@ -191,15 +183,16 @@ def tile_moe_smooth_larger_of_expert_and_shared_pl_kernel(
                 tail = ring.tile([P, J], F32, name=f"tail{t}", tag="tail")
                 lin = ring.tile([P, J], F32, name=f"lin{t}", tag="lin")
                 nc.scalar.activation(out=tail[:], in_=ex[:, J * i : J * (i + 1)], func=ACT.Ln, bias=1.0)
-                nc.scalar.activation(out=lin[:], in_=z_sb[t][:], func=ACT.Relu, scale=-1.0)
-                nc.vector.tensor_tensor(dp[t][:].indirect(offsets[:]), tail[:], lin[:], ALU.add)
+                nc.vector.scalar_tensor_tensor(out=lin[:], in0=z_sb[t][:], scalar=0.0, in1=tail[:], op0=ALU.min, op1=ALU.subtract)
+                nc.vector.tensor_copy(dp[t][:].indirect(offsets[:]), lin[:])
                 if t < PACK - 1:
-                    add(t, slice(0, T))
+                    add(nc.gpsimd, t, slice(0, BANK))
+                    add(nc.gpsimd, t, slice(BANK, T))
                     nc.sync.dma_start(out=out_rows[:, t, :], in_=y[:, t, :])
 
         last = PACK - 1
         for q in range(QUARTERS):
-            add(last, slice(q * qw, (q + 1) * qw))
+            add(nc.vector, last, slice(q * qw, (q + 1) * qw))
             if q % 2 == 1:
                 cols = slice((q - 1) * qw, (q + 1) * qw)
                 nc.sync.dma_start(out=out_rows[:, last, cols], in_=y[:, last, cols])

@@ -21,6 +21,7 @@ PACK = 4
 BANK = 512
 PASSES = K // (P * PACK)
 QUARTERS = 4
+CUT = 30.0
 
 
 def tile_moe_smooth_larger_of_expert_and_shared_pl_kernel(
@@ -34,7 +35,7 @@ def tile_moe_smooth_larger_of_expert_and_shared_pl_kernel(
 
         offsets = held.tile([P, J // 16], U16, name="offsets")
         bias = held.tile([P, PACK], F32, name="bias")
-        xt_w = held.tile([P, PASSES, 2 * T], U8, name="xt_w", align_bytes=64)
+        xt_w = [held.tile([P, 2 * T], U8, name=f"xt_w{g}", align_bytes=64) for g in range(PASSES)]
         xt_s = held.tile([P, PASSES, T], U8, name="xt_s", align_bytes=64)
         xe_w = held.tile([P, J], U32, name="xe_w", align_bytes=64)
         xe_s = held.tile([P, J], U8, name="xe_s", align_bytes=64)
@@ -48,7 +49,7 @@ def tile_moe_smooth_larger_of_expert_and_shared_pl_kernel(
         ws_s = [[held.tile([P, 2 * P], U8, name=f"ws_s{g}{a}", align_bytes=64) for a in range(2)] for g in range(PASSES)]
         p_sb = [held.tile([P, J], F32, name=f"p_sb{t}") for t in range(PACK)]
         u_sb = [held.tile([P, T], F32, name=f"u_sb{t}") for t in range(PACK)]
-        z_sb = [held.tile([P, J], F32, name=f"z_sb{t}") for t in range(PACK)]
+        z_sb = [held.tile([P, 2 * J], F32, name=f"z_sb{a}") for a in range(2)]
         dp = [held.tile([P, T], F32, name=f"dp{t}") for t in range(PACK)]
         y = held.tile([P, PACK, T], F32, name="y")
         qw = T // QUARTERS
@@ -65,18 +66,19 @@ def tile_moe_smooth_larger_of_expert_and_shared_pl_kernel(
             nc.sync.dma_start(out=ws_raw[g][:], in_=rows.rearrange("(p j) c -> p j c", j=PACK))
 
         def load_scales(tile, src):
-            for q in range(4):
-                nc.sync.dma_start(out=tile[32 * q : 32 * q + 4].bitcast(I32), in_=src[4 * q : 4 * q + 4].bitcast(I32))
+            for r in range(4):
+                nc.sync.dma_start(out=tile[r:P:32].bitcast(I32), in_=src[r:16:4].bitcast(I32))
 
         nc.sync.dma_start(out=we_w_raw[:].bitcast(I32), in_=we_words[0].bitcast(I32))
         load_scales(we_s_raw, we_scales[0])
         nc.sync.dma_start(out=xe_w[:].bitcast(I32), in_=xe_words[0].rearrange("p c r -> p (c r)").bitcast(I32))
-        nc.sync.dma_start(out=xt_w[:].bitcast(I32), in_=xt_words.rearrange("g p c -> p g c").bitcast(I32))
         load_ws(0)
         load_scales(xe_s, xe_scales[0])
-        nc.sync.dma_start(out=bias[:], in_=b.rearrange("(p t) o -> p (t o)", t=PACK))
+        nc.gpsimd.dma_start(out=bias[:], in_=b.rearrange("(p t) o -> p (t o)", t=PACK))
         load_ws(1)
         load_scales(xt_s, xt_scales.rearrange("g q c -> q g c"))
+        for g in range(PASSES):
+            nc.sync.dma_start(out=xt_w[g][:].bitcast(I32), in_=xt_words[g].bitcast(I32))
         nc.sync.dma_start(offsets[:], offs)
 
         for t in range(PACK):
@@ -132,7 +134,7 @@ def tile_moe_smooth_larger_of_expert_and_shared_pl_kernel(
                 out=u_acc[t][h][:],
                 lhsT=ws_w[g][a][:, P * i : P * (i + 1)].bitcast(FP8X4),
                 lhsT_scale=ws_s[g][a][:, P * i : P * (i + 1)],
-                rhs=xt_w[:, g, 2 * BANK * h : 2 * BANK * (h + 1)].bitcast(FP4X4),
+                rhs=xt_w[g][:, 2 * BANK * h : 2 * BANK * (h + 1)].bitcast(FP4X4),
                 rhs_scale=xt_s[:, g, BANK * h : BANK * (h + 1)],
                 start=(g == 0),
                 stop=(g == PASSES - 1),
@@ -142,8 +144,8 @@ def tile_moe_smooth_larger_of_expert_and_shared_pl_kernel(
         for t in range(PACK):
             quantize_ws(1, t)
         for t in range(PACK):
-            for g in range(PASSES):
-                for h in range(2):
+            for h in range(2):
+                for g in range(PASSES):
                     u_pass(g, t, h)
 
         def empty_u(t, h, on_vector):
@@ -153,72 +155,101 @@ def tile_moe_smooth_larger_of_expert_and_shared_pl_kernel(
             else:
                 nc.scalar.activation(out=dst, in_=u_acc[t][h][:], func=ACT.Identity, bias=bias[:, t : t + 1])
 
+        def z_of(t):
+            a, i = divmod(t, 2)
+            return z_sb[a][:, J * i : J * (i + 1)]
+
         def gather(t):
-            nc.vector.tensor_tensor(z_sb[t][:], u_sb[t][:].indirect(offsets[:]), p_sb[t][:], ALU.subtract)
+            nc.vector.tensor_tensor(z_of(t), u_sb[t][:].indirect(offsets[:]), p_sb[t][:], ALU.subtract)
+
+        def cap(a):
+            capped = held.tile([P, 2 * J], F32, name=f"capped{a}", tag="capped")
+            if a == 0:
+                nc.vector.tensor_scalar(out=capped[:], in0=z_sb[a][:], scalar1=CUT, scalar2=0.0, op0=ALU.add, op1=ALU.max)
+            else:
+                nc.scalar.activation(out=capped[:], in_=z_sb[a][:], func=ACT.Relu, bias=CUT)
+            return capped
 
         empty_u(0, 0, False)
         empty_u(0, 1, True)
         empty_u(1, 0, False)
         empty_u(1, 1, False)
+        empty_u(2, 0, False)
+        empty_u(2, 1, False)
+        empty_u(3, 0, False)
         gather(0)
         gather(1)
-        for t in (2, 3):
-            empty_u(t, 0, True)
-            empty_u(t, 1, True)
-            gather(t)
+        capped = cap(0)
+        gather(2)
+        empty_u(3, 1, True)
+        gather(3)
 
         out_rows = out_0.rearrange("(p t) c -> p t c", t=PACK)
 
         def add(engine, t, cols):
-            engine.tensor_tensor(y[:, t, cols], u_sb[t][:, cols], dp[t][:, cols], ALU.subtract)
+            engine.tensor_tensor(y[:, t, cols], u_sb[t][:, cols], dp[t][:, cols], ALU.add)
+
+        def round_y(q, a, on_vector, part):
+            src = y[:, 2 * a : 2 * a + 2, q * qw : (q + 1) * qw].rearrange("p t c -> p c t")[:, part]
+            dst = y_bf[q][:].rearrange("p (c t) -> p c t", t=PACK)[:, part, 2 * a : 2 * a + 2]
+            if on_vector:
+                nc.vector.tensor_copy(out=dst, in_=src)
+            else:
+                nc.scalar.copy(out=dst, in_=src)
 
         for a in range(2):
-            mag = held.tile([P, 2 * J], F32, name=f"mag{a}", tag="mag")
+            if a == 1:
+                capped = cap(1)
             ex = held.tile([P, 2 * J], F32, name=f"ex{a}", tag="ex")
-            for i in range(2):
-                nc.scalar.activation(out=mag[:, J * i : J * (i + 1)], in_=z_sb[2 * a + i][:], func=ACT.Abs)
-            nc.scalar.activation(out=ex[:], in_=mag[:], func=ACT.Exp, scale=-1.0)
+            nc.scalar.activation(out=ex[:], in_=capped[:], func=ACT.Exp, scale=-1.0, bias=CUT)
             for i in range(2):
                 t = 2 * a + i
-                tail = ring.tile([P, J], F32, name=f"tail{t}", tag="tail")
-                lin = ring.tile([P, J], F32, name=f"lin{t}", tag="lin")
-                nc.scalar.activation(out=tail[:], in_=ex[:, J * i : J * (i + 1)], func=ACT.Ln, bias=1.0)
-                nc.vector.scalar_tensor_tensor(out=lin[:], in0=z_sb[t][:], scalar=0.0, in1=tail[:], op0=ALU.min, op1=ALU.subtract)
-                nc.vector.tensor_copy(dp[t][:].indirect(offsets[:]), lin[:])
+                soft = ring.tile([P, J], F32, name=f"soft{t}", tag="soft")
+                d = ring.tile([P, J], F32, name=f"d{t}", tag="d")
+                nc.scalar.activation(out=soft[:], in_=ex[:, J * i : J * (i + 1)], func=ACT.Ln, bias=1.0)
+                nc.vector.scalar_tensor_tensor(out=d[:], in0=z_of(t), scalar=-1.0, in1=soft[:], op0=ALU.mult, op1=ALU.max)
+                nc.vector.tensor_copy(dp[t][:].indirect(offsets[:]), d[:])
                 if t < PACK - 1:
                     add(nc.gpsimd, t, slice(0, BANK))
                     add(nc.gpsimd, t, slice(BANK, T))
                     nc.sync.dma_start(out=out_rows[:, t, :], in_=y[:, t, :])
 
-        last = PACK - 1
+        whole = slice(0, qw)
         for q in range(QUARTERS):
-            add(nc.vector, last, slice(q * qw, (q + 1) * qw))
-            if q % 2 == 1:
-                cols = slice((q - 1) * qw, (q + 1) * qw)
-                nc.sync.dma_start(out=out_rows[:, last, cols], in_=y[:, last, cols])
+            round_y(q, 0, False, whole)
 
-        def round_y(q):
-            src = y[:, :, q * qw : (q + 1) * qw].rearrange("p t (c i) -> p c t i", i=4)
-            dst = y_bf[q][:].rearrange("p (c i t) -> p c t i", i=4, t=PACK)
-            if q < 2:
-                nc.scalar.copy(out=dst, in_=src)
-            else:
-                nc.vector.tensor_copy(out=dst, in_=src)
+        last = PACK - 1
+        add(nc.gpsimd, last, slice(3 * qw, 4 * qw))
+        for q in range(3):
+            h, i = divmod(q, 2)
+            cols = slice(q * qw, (q + 1) * qw)
+            nc.vector.scalar_tensor_tensor(
+                out=y[:, last, cols], in0=u_acc[last][h][:, i * qw : (i + 1) * qw], scalar=bias[:, last : last + 1],
+                in1=dp[last][:, cols], op0=ALU.add, op1=ALU.add,
+            )
+        nc.sync.dma_start(out=out_rows[:, last, :], in_=y[:, last, :])
 
         words_out = out_1[0].rearrange("p c r -> p (c r)").bitcast(I32)
 
         def quantize_y(q):
             cols = slice(q * qw, (q + 1) * qw)
             nc.vector.quantize_mx(out=y_w[:, cols].bitcast(FP8X4), scales=y_s[:, cols], in_=y_bf[q][:])
+
+        def store_words(cols):
             nc.sync.dma_start(out=words_out[:, cols], in_=y_w[:, cols].bitcast(I32))
 
-        round_y(0)
-        round_y(1)
-        round_y(2)
+        round_y(0, 1, False, whole)
+        round_y(1, 1, False, whole)
+        round_y(2, 1, False, slice(0, qw // 2))
+        round_y(3, 1, True, whole)
+        round_y(2, 1, True, slice(qw // 2, qw))
         quantize_y(0)
-        round_y(3)
-        quantize_y(2)
-        quantize_y(1)
         quantize_y(3)
+        store_words(slice(3 * qw, 4 * qw))
+        quantize_y(1)
+        store_words(slice(0, 2 * qw))
+        quantize_y(2)
+        store_words(slice(2 * qw, 3 * qw))
         for q in range(4):
-            nc.scalar.dma_start(out=out_2[0, 4 * q : 4 * q + 4, :].bitcast(I32), in_=y_s[32 * q : 32 * q + 4, :].bitcast(I32))
+            queue = nc.scalar if q < 2 else nc.sync
+            queue.dma_start(out=out_2[0, q:16:4, :].bitcast(I32), in_=y_s[q:P:32, :].bitcast(I32))

@@ -73,12 +73,12 @@ def tile_moe_smooth_larger_of_expert_and_shared_pl_kernel(
         load_scales(we_s_raw, we_scales[0])
         nc.sync.dma_start(out=xe_w[:].bitcast(I32), in_=xe_words[0].rearrange("p c r -> p (c r)").bitcast(I32))
         load_ws(0)
+        nc.sync.dma_start(out=xt_w[0][:].bitcast(I32), in_=xt_words[0].bitcast(I32))
         load_scales(xe_s, xe_scales[0])
-        nc.gpsimd.dma_start(out=bias[:], in_=b.rearrange("(p t) o -> p (t o)", t=PACK))
+        nc.sync.dma_start(out=bias[:], in_=b.rearrange("(p t) o -> p (t o)", t=PACK))
         load_ws(1)
         load_scales(xt_s, xt_scales.rearrange("g q c -> q g c"))
-        for g in range(PASSES):
-            nc.sync.dma_start(out=xt_w[g][:].bitcast(I32), in_=xt_words[g].bitcast(I32))
+        nc.sync.dma_start(out=xt_w[1][:].bitcast(I32), in_=xt_words[1].bitcast(I32))
         nc.sync.dma_start(offsets[:], offs)
 
         for t in range(PACK):
@@ -189,9 +189,9 @@ def tile_moe_smooth_larger_of_expert_and_shared_pl_kernel(
         def add(engine, t, cols):
             engine.tensor_tensor(y[:, t, cols], u_sb[t][:, cols], dp[t][:, cols], ALU.add)
 
-        def round_y(q, a, on_vector, part):
-            src = y[:, 2 * a : 2 * a + 2, q * qw : (q + 1) * qw].rearrange("p t c -> p c t")[:, part]
-            dst = y_bf[q][:].rearrange("p (c t) -> p c t", t=PACK)[:, part, 2 * a : 2 * a + 2]
+        def round_y(q, on_vector):
+            src = y[:, :, q * qw : (q + 1) * qw].rearrange("p t (c i) -> p c t i", i=4)
+            dst = y_bf[q][:].rearrange("p (c i t) -> p c t i", i=4, t=PACK)
             if on_vector:
                 nc.vector.tensor_copy(out=dst, in_=src)
             else:
@@ -214,19 +214,9 @@ def tile_moe_smooth_larger_of_expert_and_shared_pl_kernel(
                     add(nc.gpsimd, t, slice(BANK, T))
                     nc.sync.dma_start(out=out_rows[:, t, :], in_=y[:, t, :])
 
-        whole = slice(0, qw)
-        for q in range(QUARTERS):
-            round_y(q, 0, False, whole)
-
         last = PACK - 1
-        add(nc.gpsimd, last, slice(3 * qw, 4 * qw))
-        for q in range(3):
-            h, i = divmod(q, 2)
-            cols = slice(q * qw, (q + 1) * qw)
-            nc.vector.scalar_tensor_tensor(
-                out=y[:, last, cols], in0=u_acc[last][h][:, i * qw : (i + 1) * qw], scalar=bias[:, last : last + 1],
-                in1=dp[last][:, cols], op0=ALU.add, op1=ALU.add,
-            )
+        for q in range(QUARTERS):
+            add(nc.vector, last, slice(q * qw, (q + 1) * qw))
         nc.sync.dma_start(out=out_rows[:, last, :], in_=y[:, last, :])
 
         words_out = out_1[0].rearrange("p c r -> p (c r)").bitcast(I32)
@@ -238,18 +228,17 @@ def tile_moe_smooth_larger_of_expert_and_shared_pl_kernel(
         def store_words(cols):
             nc.sync.dma_start(out=words_out[:, cols], in_=y_w[:, cols].bitcast(I32))
 
-        round_y(0, 1, False, whole)
-        round_y(1, 1, False, whole)
-        round_y(2, 1, False, slice(0, qw // 2))
-        round_y(3, 1, True, whole)
-        round_y(2, 1, True, slice(qw // 2, qw))
+        round_y(0, False)
+        round_y(1, False)
+        round_y(2, True)
         quantize_y(0)
-        quantize_y(3)
-        store_words(slice(3 * qw, 4 * qw))
-        quantize_y(1)
-        store_words(slice(0, 2 * qw))
+        round_y(3, True)
         quantize_y(2)
         store_words(slice(2 * qw, 3 * qw))
+        quantize_y(1)
+        store_words(slice(0, 2 * qw))
+        quantize_y(3)
+        store_words(slice(3 * qw, 4 * qw))
         for q in range(4):
             queue = nc.scalar if q < 2 else nc.sync
             queue.dma_start(out=out_2[0, q:16:4, :].bitcast(I32), in_=y_s[q:P:32, :].bitcast(I32))

from contextlib import ExitStack

import concourse.mybir as mybir

K, L, T, J, N = 1024, 512, 1024, 512, 512
FLOPS = 2 * K * N * T + 2 * L * N * J

F32 = mybir.dt.float32
BF16 = mybir.dt.bfloat16
I32 = mybir.dt.int32
U32 = mybir.dt.uint32
U16 = mybir.dt.uint16
U8 = mybir.dt.uint8
FP8X4 = mybir.dt.float8_e4m3fn_x4
FP4X4 = mybir.dt.float4_e2m1fn_x4
ACT = mybir.ActivationFunctionType
ALU = mybir.AluOpType

P = 128
PACK = 4
BANK = 512
PASSES = K // (P * PACK)
QUARTERS = 4
CUT = 30.0


def tile_moe_smooth_larger_of_expert_and_shared_pl_kernel(
    tc, xt_words, xt_scales, ws, xe_words, xe_scales, we_words, we_scales, b, offs, out_0, out_1, out_2
):
    nc = tc.nc
    with ExitStack() as ctx:
        held = ctx.enter_context(tc.tile_pool(name="held", bufs=1))
        ring = ctx.enter_context(tc.tile_pool(name="ring", bufs=2))
        psum = ctx.enter_context(tc.psum_pool(name="psum", bufs=1))

        offsets = held.tile([P, J // 16], U16, name="offsets")
        bias = held.tile([P, PACK], F32, name="bias")
        xt_w = [held.tile([P, 2 * T], U8, name=f"xt_w{g}", align_bytes=64) for g in range(PASSES)]
        xt_s = held.tile([P, PASSES, T], U8, name="xt_s", align_bytes=64)
        xe_w = held.tile([P, J], U32, name="xe_w", align_bytes=64)
        xe_s = held.tile([P, J], U8, name="xe_s", align_bytes=64)
        we_w_raw = held.tile([P, 2 * N], U8, name="we_w_raw", align_bytes=64)
        we_s_raw = held.tile([P, N], U8, name="we_s_raw", align_bytes=64)
        we_w = held.tile([P, 2 * N], U8, name="we_w", align_bytes=64)
        we_s = held.tile([P, N], U8, name="we_s", align_bytes=64)
        ws_raw = [held.tile([P, PACK, N], F32, name=f"ws_raw{g}") for g in range(PASSES)]
        ws_bf = [[held.tile([P, 2 * P * PACK], BF16, name=f"ws_bf{g}{a}", align_bytes=64) for a in range(2)] for g in range(PASSES)]
        ws_w = [[held.tile([P, 2 * P], U32, name=f"ws_w{g}{a}", align_bytes=64) for a in range(2)] for g in range(PASSES)]
        ws_s = [[held.tile([P, 2 * P], U8, name=f"ws_s{g}{a}", align_bytes=64) for a in range(2)] for g in range(PASSES)]
        p_sb = [held.tile([P, J], F32, name=f"p_sb{t}") for t in range(PACK)]
        u_sb = [held.tile([P, T], F32, name=f"u_sb{t}") for t in range(PACK)]
        z_sb = [held.tile([P, 2 * J], F32, name=f"z_sb{a}") for a in range(2)]
        dp = [held.tile([P, T], F32, name=f"dp{t}") for t in range(PACK)]
        y = held.tile([P, PACK, T], F32, name="y")
        qw = T // QUARTERS
        y_bf = [held.tile([P, qw * PACK], BF16, name=f"y_bf{q}", align_bytes=64) for q in range(QUARTERS)]
        y_w = held.tile([P, T], U32, name="y_w", align_bytes=64)
        y_s = held.tile([P, T], U8, name="y_s", align_bytes=64)

        nc.gpsimd.memset(we_s_raw[:].bitcast(I32), 0)
        nc.gpsimd.memset(xe_s[:].bitcast(I32), 0)
        nc.gpsimd.memset(xt_s[:].rearrange("p g c -> p (g c)").bitcast(I32), 0)

        def load_ws(g):
            rows = ws[g * P * PACK : (g + 1) * P * PACK, :]
            nc.sync.dma_start(out=ws_raw[g][:], in_=rows.rearrange("(p j) c -> p j c", j=PACK))

        def load_scales(tile, src):
            for r in range(4):
                nc.sync.dma_start(out=tile[r:P:32].bitcast(I32), in_=src[r:16:4].bitcast(I32))

        nc.sync.dma_start(out=we_w_raw[:].bitcast(I32), in_=we_words[0].bitcast(I32))
        load_scales(we_s_raw, we_scales[0])
        nc.sync.dma_start(out=xe_w[:].bitcast(I32), in_=xe_words[0].rearrange("p c r -> p (c r)").bitcast(I32))
        load_ws(0)
        nc.sync.dma_start(out=xt_w[0][:].bitcast(I32), in_=xt_words[0].bitcast(I32))
        load_scales(xe_s, xe_scales[0])
        nc.sync.dma_start(out=bias[:], in_=b.rearrange("(p t) o -> p (t o)", t=PACK))
        load_ws(1)
        load_scales(xt_s, xt_scales.rearrange("g q c -> q g c"))
        nc.sync.dma_start(out=xt_w[1][:].bitcast(I32), in_=xt_words[1].bitcast(I32))
        nc.sync.dma_start(offsets[:], offs)

        for t in range(PACK):
            nc.vector.memset(dp[t][:], 0.0)

        nc.vector.tensor_copy(
            out=we_w[:].rearrange("p (t m e) -> p t m e", t=PACK, e=2),
            in_=we_w_raw[:].rearrange("p (m t e) -> p t m e", t=PACK, e=2),
        )
        nc.vector.tensor_copy(
            out=we_s[:].rearrange("p (t m) -> p t m", t=PACK),
            in_=we_s_raw[:].rearrange("p (m t) -> p t m", t=PACK),
        )

        def round_ws(g):
            src = ws_raw[g][:].rearrange("p j (m t) -> p m j t", t=PACK)
            for a in range(2):
                dst = ws_bf[g][a][:].rearrange("p (t m j) -> p m j t", t=2, j=PACK)
                if a == 0:
                    nc.vector.tensor_copy(out=dst, in_=src[:, :, :, 0:2])
                else:
                    nc.scalar.copy(out=dst, in_=src[:, :, :, 2:4])

        def quantize_ws(g, t):
            a, i = divmod(t, 2)
            cols = slice(P * i, P * (i + 1))
            nc.vector.quantize_mx(
                out=ws_w[g][a][:, cols].bitcast(FP8X4), scales=ws_s[g][a][:, cols], in_=ws_bf[g][a][:, PACK * P * i : PACK * P * (i + 1)]
            )

        round_ws(0)
        for t in range(PACK):
            quantize_ws(0, t)

        for t in range(PACK):
            acc = psum.tile([P, BANK], F32, name=f"p_acc{t}", tag=f"bank{4 + t}")
            nc.tensor.matmul_mx(
                out=acc[:],
                lhsT=we_w[:, 2 * P * t : 2 * P * (t + 1)].bitcast(FP4X4),
                lhsT_scale=we_s[:, P * t : P * (t + 1)],
                rhs=xe_w[:].bitcast(FP8X4),
                rhs_scale=xe_s[:],
                start=True,
                stop=True,
            )
            nc.scalar.activation(out=p_sb[t][:], in_=acc[:], func=ACT.Identity, bias=bias[:, t : t + 1])

        u_acc = [[psum.tile([P, BANK], F32, name=f"u_acc{t}{h}", tag=f"bank{2 * t + h}") for h in range(2)] for t in range(PACK)]

        def u_pass(g, t, h):
            a, i = divmod(t, 2)
            nc.tensor.matmul_mx(
                out=u_acc[t][h][:],
                lhsT=ws_w[g][a][:, P * i : P * (i + 1)].bitcast(FP8X4),
                lhsT_scale=ws_s[g][a][:, P * i : P * (i + 1)],
                rhs=xt_w[g][:, 2 * BANK * h : 2 * BANK * (h + 1)].bitcast(FP4X4),
                rhs_scale=xt_s[:, g, BANK * h : BANK * (h + 1)],
                start=(g == 0),
                stop=(g == PASSES - 1),
            )

        round_ws(1)
        for t in range(PACK):
            quantize_ws(1, t)
        for t in range(PACK):
            for h in range(2):
                for g in range(PASSES):
                    u_pass(g, t, h)

        def empty_u(t, h, on_vector):
            dst = u_sb[t][:, BANK * h : BANK * (h + 1)]
            if on_vector:
                nc.vector.tensor_scalar(out=dst, in0=u_acc[t][h][:], scalar1=bias[:, t : t + 1], scalar2=None, op0=ALU.add)
            else:
                nc.scalar.activation(out=dst, in_=u_acc[t][h][:], func=ACT.Identity, bias=bias[:, t : t + 1])

        def z_of(t):
            a, i = divmod(t, 2)
            return z_sb[a][:, J * i : J * (i + 1)]

        def gather(t):
            nc.vector.tensor_tensor(z_of(t), u_sb[t][:].indirect(offsets[:]), p_sb[t][:], ALU.subtract)

        def cap(a):
            capped = held.tile([P, 2 * J], F32, name=f"capped{a}", tag="capped")
            if a == 0:
                nc.vector.tensor_scalar(out=capped[:], in0=z_sb[a][:], scalar1=CUT, scalar2=0.0, op0=ALU.add, op1=ALU.max)
            else:
                nc.scalar.activation(out=capped[:], in_=z_sb[a][:], func=ACT.Relu, bias=CUT)
            return capped

        empty_u(0, 0, False)
        empty_u(0, 1, True)
        empty_u(1, 0, False)
        empty_u(1, 1, False)
        empty_u(2, 0, False)
        empty_u(2, 1, False)
        empty_u(3, 0, False)
        gather(0)
        gather(1)
        capped = cap(0)
        gather(2)
        empty_u(3, 1, True)
        gather(3)

        out_rows = out_0.rearrange("(p t) c -> p t c", t=PACK)

        def add(engine, t, cols):
            engine.tensor_tensor(y[:, t, cols], u_sb[t][:, cols], dp[t][:, cols], ALU.add)

        def round_y(q, on_vector):
            src = y[:, :, q * qw : (q + 1) * qw].rearrange("p t (c i) -> p c t i", i=4)
            dst = y_bf[q][:].rearrange("p (c i t) -> p c t i", i=4, t=PACK)
            if on_vector:
                nc.vector.tensor_copy(out=dst, in_=src)
            else:
                nc.scalar.copy(out=dst, in_=src)

        for a in range(2):
            if a == 1:
                capped = cap(1)
            ex = held.tile([P, 2 * J], F32, name=f"ex{a}", tag="ex")
            nc.scalar.activation(out=ex[:], in_=capped[:], func=ACT.Exp, scale=-1.0, bias=CUT)
            for i in range(2):
                t = 2 * a + i
                soft = ring.tile([P, J], F32, name=f"soft{t}", tag="soft")
                d = ring.tile([P, J], F32, name=f"d{t}", tag="d")
                nc.scalar.activation(out=soft[:], in_=ex[:, J * i : J * (i + 1)], func=ACT.Ln, bias=1.0)
                nc.vector.scalar_tensor_tensor(out=d[:], in0=z_of(t), scalar=-1.0, in1=soft[:], op0=ALU.mult, op1=ALU.max)
                nc.vector.tensor_copy(dp[t][:].indirect(offsets[:]), d[:])
                if t < PACK - 1:
                    add(nc.gpsimd, t, slice(0, BANK))
                    add(nc.gpsimd, t, slice(BANK, T))
                    nc.sync.dma_start(out=out_rows[:, t, :], in_=y[:, t, :])

        last = PACK - 1
        for q in range(QUARTERS):
            add(nc.vector, last, slice(q * qw, (q + 1) * qw))
        nc.sync.dma_start(out=out_rows[:, last, :], in_=y[:, last, :])

        words_out = out_1[0].rearrange("p c r -> p (c r)").bitcast(I32)

        def quantize_y(q):
            cols = slice(q * qw, (q + 1) * qw)
            nc.vector.quantize_mx(out=y_w[:, cols].bitcast(FP8X4), scales=y_s[:, cols], in_=y_bf[q][:])

        def store_words(cols):
            nc.sync.dma_start(out=words_out[:, cols], in_=y_w[:, cols].bitcast(I32))

        round_y(0, False)
        round_y(1, False)
        round_y(2, True)
        quantize_y(0)
        round_y(3, True)
        quantize_y(2)
        store_words(slice(2 * qw, 3 * qw))
        quantize_y(1)
        store_words(slice(0, 2 * qw))
        quantize_y(3)
        store_words(slice(3 * qw, 4 * qw))
        for q in range(4):
            queue = nc.scalar if q < 2 else nc.sync
            queue.dma_start(out=out_2[0, q:16:4, :].bitcast(I32), in_=y_s[q:P:32, :].bitcast(I32))
